import numpy as np
import ml_dtypes

BF16 = ml_dtypes.bfloat16


def bf(x):
    return np.asarray(x, np.float32).astype(BF16)


def f32(x):
    return np.asarray(x, np.float32)


def f64(x):
    return np.asarray(x).astype(np.float64)


def striped(idx):
    return np.tile(idx.reshape(-1, 16).T, (8, 1))


def rows(idx, k):
    return np.tile(idx, (k, 1))


def look(tab, idx):
    return np.take_along_axis(f64(tab), rows(idx, len(tab)), axis=1)


K, S, D, V, N, M = 512, 2048, 2, 1024, 2048, 512


def setup_inputs():
    return {"tab": f32(np.random.standard_normal((K, S))), "x0": f32(1.0 * np.random.standard_normal((K, V))), "w": bf(np.random.standard_normal((K, M)) / np.sqrt(K)), "b": f32(0.5 * np.random.standard_normal((M, 1))), "offs": striped(np.random.permutation(S)[:N])}


def reference(tab, x0, w, b, offs):
    idx = offs[:16].T.reshape(-1)
    hi = lo = f64(x0)
    for d in range(D):
        hi, lo = np.maximum(hi, look(tab, idx[d * V:(d + 1) * V])), np.minimum(lo, look(tab, idx[d * V:(d + 1) * V]))
    x = hi - lo
    return np.maximum(f64(w).T @ x + f64(b), 0.0)

@@ -1,0 +1,81 @@
+import concourse.mybir as mybir
+
+F32, BF16, U16 = mybir.dt.float32, mybir.dt.bfloat16, mybir.dt.uint16
+MAX, MIN, SUBTRACT = mybir.AluOpType.max, mybir.AluOpType.min, mybir.AluOpType.subtract
+RELU = mybir.ActivationFunctionType.Relu
+
+P = 128
+ROWS, COLS = 512, 2048
+V = 1024
+M = 512
+BLOCKS = ROWS // P
+GROUPS = M // P
+PER_COLUMN = 16
+BANK = 512
+
+FLOPS = 2 * ROWS * M * V
+
+
+def tile_lookup_span_relu_kernel(tc, tab, x0, w, b, offs, out):
+    nc = tc.nc
+    with (
+        tc.tile_pool(name="held", bufs=1) as held,
+        tc.tile_pool(name="tables", bufs=BLOCKS) as tables,
+        tc.tile_pool(name="work", bufs=2) as work,
+        tc.psum_pool(name="psum", bufs=1) as psum,
+    ):
+        offsets = held.tile([P, 2 * V // PER_COLUMN], U16, name="offsets")
+        nc.sync.dma_start(offsets[:], offs)
+        first_neighbour = offsets[:, : V // PER_COLUMN]
+        second_neighbour = offsets[:, V // PER_COLUMN :]
+
+        windows, owns = [], []
+        for k in range(BLOCKS):
+            rows = slice(k * P, (k + 1) * P)
+            window = tables.tile([P, COLS], F32, name="window")
+            own = tables.tile([P, V], F32, name="own")
+            if k == 0:
+                nc.scalar.dma_start(window[:, : COLS // 2], tab[rows, : COLS // 2])
+                nc.sync.dma_start(window[:, COLS // 2 :], tab[rows, COLS // 2 :])
+            else:
+                nc.sync.dma_start(window[:], tab[rows, :])
+            nc.scalar.dma_start(own[:], x0[rows, :])
+            windows.append(window)
+            owns.append(own)
+
+        weights = held.tile([P, BLOCKS, M], BF16, name="weights")
+        nc.scalar.dma_start(weights[:], w.rearrange("(k p) m -> p k m", p=P))
+        bias = held.tile([P, GROUPS], F32, name="bias")
+        with nc.allow_non_contiguous_dma(reason="512 single values, once"):
+            nc.scalar.dma_start(bias[:], b.rearrange("(g p) one -> p (g one)", p=P))
+
+        sums = [
+            [psum.tile([P, BANK], F32, name=f"sum_{g}_{h}") for h in range(V // BANK)] for g in range(GROUPS)
+        ]
+        for k in range(BLOCKS):
+            window, own = windows[k], owns[k]
+            high1 = work.tile([P, V], F32, name="high1")
+            low1 = work.tile([P, V], F32, name="low1")
+            high2 = work.tile([P, V], F32, name="high2")
+            low2 = work.tile([P, V], F32, name="low2")
+            nc.vector.tensor_tensor(high1[:], window[:].indirect(first_neighbour), own[:], MAX)
+            nc.vector.tensor_tensor(low1[:], window[:].indirect(first_neighbour), own[:], MIN)
+            nc.vector.tensor_tensor(high2[:], window[:].indirect(second_neighbour), high1[:], MAX)
+            nc.vector.tensor_tensor(low2[:], window[:].indirect(second_neighbour), low1[:], MIN)
+            span = work.tile([P, V], BF16, name="span")
+            nc.vector.tensor_tensor(span[:], high2[:], low2[:], SUBTRACT)
+            for g in range(GROUPS):
+                for h in range(V // BANK):
+                    nc.tensor.matmul(
+                        sums[g][h][:],
+                        weights[:, k, g * P : (g + 1) * P],
+                        span[:, h * BANK : (h + 1) * BANK],
+                        start=(k == 0),
+                        stop=(k == BLOCKS - 1),
+                    )
+
+        for g in range(GROUPS):
+            result = work.tile([P, V], F32, name="result")
+            for h in range(V // BANK):
+                nc.scalar.activation(result[:, h * BANK : (h + 1) * BANK], sums[g][h][:], RELU, bias=bias[:, g : g + 1])
+            nc.sync.dma_start(out[g * P : (g + 1) * P, :], result[:])

@@ -2,6 +2,7 @@ import concourse.mybir as mybir
 
 F32, BF16, U16 = mybir.dt.float32, mybir.dt.bfloat16, mybir.dt.uint16
 MAX, MIN, SUBTRACT = mybir.AluOpType.max, mybir.AluOpType.min, mybir.AluOpType.subtract
+ADD = mybir.AluOpType.add
 RELU = mybir.ActivationFunctionType.Relu
 
 P = 128
@@ -13,6 +14,8 @@ GROUPS = M // P
 PER_COLUMN = 16
 BANK = 512
 
+PIECES = ((0, BANK), (BANK, BANK // 2), (BANK + BANK // 2, BANK // 2))
+
 FLOPS = 2 * ROWS * M * V
 
 
@@ -20,20 +23,19 @@ def tile_lookup_span_relu_kernel(tc, tab, x0, w, b, offs, out):
     nc = tc.nc
     with (
         tc.tile_pool(name="held", bufs=1) as held,
-        tc.tile_pool(name="tables", bufs=BLOCKS) as tables,
+        tc.tile_pool(name="blocks", bufs=BLOCKS) as blocks,
         tc.tile_pool(name="work", bufs=2) as work,
-        tc.psum_pool(name="psum", bufs=1) as psum,
+        tc.tile_pool(name="results", bufs=2 * GROUPS) as results,
+        tc.psum_pool(name="psum", bufs=2 * GROUPS) as psum,
     ):
         offsets = held.tile([P, 2 * V // PER_COLUMN], U16, name="offsets")
         nc.sync.dma_start(offsets[:], offs)
-        first_neighbour = offsets[:, : V // PER_COLUMN]
-        second_neighbour = offsets[:, V // PER_COLUMN :]
 
         windows, owns = [], []
         for k in range(BLOCKS):
             rows = slice(k * P, (k + 1) * P)
-            window = tables.tile([P, COLS], F32, name="window")
-            own = tables.tile([P, V], F32, name="own")
+            window = blocks.tile([P, COLS], F32, name="window")
+            own = blocks.tile([P, V], F32, name="own")
             if k == 0:
                 nc.scalar.dma_start(window[:, : COLS // 2], tab[rows, : COLS // 2])
                 nc.sync.dma_start(window[:, COLS // 2 :], tab[rows, COLS // 2 :])
@@ -49,33 +51,42 @@ def tile_lookup_span_relu_kernel(tc, tab, x0, w, b, offs, out):
         with nc.allow_non_contiguous_dma(reason="512 single values, once"):
             nc.scalar.dma_start(bias[:], b.rearrange("(g p) one -> p (g one)", p=P))
 
-        sums = [
-            [psum.tile([P, BANK], F32, name=f"sum_{g}_{h}") for h in range(V // BANK)] for g in range(GROUPS)
-        ]
-        for k in range(BLOCKS):
-            window, own = windows[k], owns[k]
+        spans = [blocks.tile([P, V], BF16, name="span") for k in range(BLOCKS)]
+
+        def look_up(k, start, width):
+            nodes = slice(start, start + width)
+            first = offsets[:, start // PER_COLUMN : (start + width) // PER_COLUMN]
+            second = offsets[:, (V + start) // PER_COLUMN : (V + start + width) // PER_COLUMN]
             high1 = work.tile([P, V], F32, name="high1")
             low1 = work.tile([P, V], F32, name="low1")
             high2 = work.tile([P, V], F32, name="high2")
             low2 = work.tile([P, V], F32, name="low2")
-            nc.vector.tensor_tensor(high1[:], window[:].indirect(first_neighbour), own[:], MAX)
-            nc.vector.tensor_tensor(low1[:], window[:].indirect(first_neighbour), own[:], MIN)
-            nc.vector.tensor_tensor(high2[:], window[:].indirect(second_neighbour), high1[:], MAX)
-            nc.vector.tensor_tensor(low2[:], window[:].indirect(second_neighbour), low1[:], MIN)
-            span = work.tile([P, V], BF16, name="span")
-            nc.vector.tensor_tensor(span[:], high2[:], low2[:], SUBTRACT)
-            for g in range(GROUPS):
-                for h in range(V // BANK):
+            nc.vector.tensor_tensor(high1[:, :width], windows[k][:].indirect(first), owns[k][:, nodes], MAX)
+            nc.vector.tensor_tensor(low1[:, :width], windows[k][:].indirect(first), owns[k][:, nodes], MIN)
+            nc.vector.tensor_tensor(high2[:, :width], windows[k][:].indirect(second), high1[:, :width], MAX)
+            nc.vector.tensor_tensor(low2[:, :width], windows[k][:].indirect(second), low1[:, :width], MIN)
+            nc.vector.tensor_tensor(spans[k][:, nodes], high2[:, :width], low2[:, :width], SUBTRACT)
+
+        for k in range(BLOCKS - 1):
+            look_up(k, 0, V)
+
+        for start, width in PIECES:
+            look_up(BLOCKS - 1, start, width)
+            nodes = slice(start, start + width)
+            sums = [psum.tile([P, BANK], F32, name="sum") for g in range(GROUPS)]
+            for k in range(BLOCKS):
+                for g in range(GROUPS):
                     nc.tensor.matmul(
-                        sums[g][h][:],
+                        sums[g][:, :width],
                         weights[:, k, g * P : (g + 1) * P],
-                        span[:, h * BANK : (h + 1) * BANK],
+                        spans[k][:, nodes],
                         start=(k == 0),
                         stop=(k == BLOCKS - 1),
                     )
-
-        for g in range(GROUPS):
-            result = work.tile([P, V], F32, name="result")
-            for h in range(V // BANK):
-                nc.scalar.activation(result[:, h * BANK : (h + 1) * BANK], sums[g][h][:], RELU, bias=bias[:, g : g + 1])
-            nc.sync.dma_start(out[g * P : (g + 1) * P, :], result[:])
+            for g in range(GROUPS):
+                result = results.tile([P, BANK], F32, name="result")
+                if start + width == V and g % 2 == 1:
+                    nc.vector.tensor_scalar(result[:, :width], sums[g][:, :width], bias[:, g : g + 1], 0.0, ADD, MAX)
+                else:
+                    nc.scalar.activation(result[:, :width], sums[g][:, :width], RELU, bias=bias[:, g : g + 1])
+                nc.sync.dma_start(out[g * P : (g + 1) * P, nodes], result[:, :width])

@@ -1,9 +1,10 @@
 import concourse.mybir as mybir
+from concourse.masks import make_identity
 
 F32, BF16, U16 = mybir.dt.float32, mybir.dt.bfloat16, mybir.dt.uint16
 MAX, MIN, SUBTRACT = mybir.AluOpType.max, mybir.AluOpType.min, mybir.AluOpType.subtract
 ADD = mybir.AluOpType.add
-RELU = mybir.ActivationFunctionType.Relu
+COPY, RELU = mybir.ActivationFunctionType.Copy, mybir.ActivationFunctionType.Relu
 
 P = 128
 ROWS, COLS = 512, 2048
@@ -26,7 +27,8 @@ def tile_lookup_span_relu_kernel(tc, tab, x0, w, b, offs, out):
         tc.tile_pool(name="blocks", bufs=BLOCKS) as blocks,
         tc.tile_pool(name="work", bufs=2) as work,
         tc.tile_pool(name="results", bufs=2 * GROUPS) as results,
-        tc.psum_pool(name="psum", bufs=2 * GROUPS) as psum,
+        tc.psum_pool(name="differences", bufs=2) as differences,
+        tc.psum_pool(name="psum", bufs=6) as psum,
     ):
         offsets = held.tile([P, 2 * V // PER_COLUMN], U16, name="offsets")
         nc.sync.dma_start(offsets[:], offs)
@@ -51,6 +53,11 @@ def tile_lookup_span_relu_kernel(tc, tab, x0, w, b, offs, out):
         with nc.allow_non_contiguous_dma(reason="512 single values, once"):
             nc.scalar.dma_start(bias[:], b.rearrange("(g p) one -> p (g one)", p=P))
 
+        plus = held.tile([P, P], F32, name="plus")
+        minus = held.tile([P, P], F32, name="minus")
+        make_identity(nc, plus[:])
+        nc.gpsimd.tensor_scalar_mul(minus[:], plus[:], -1.0)
+
         spans = [blocks.tile([P, V], BF16, name="span") for k in range(BLOCKS)]
 
         def look_up(k, start, width):
@@ -65,7 +72,15 @@ def tile_lookup_span_relu_kernel(tc, tab, x0, w, b, offs, out):
             nc.vector.tensor_tensor(low1[:, :width], windows[k][:].indirect(first), owns[k][:, nodes], MIN)
             nc.vector.tensor_tensor(high2[:, :width], windows[k][:].indirect(second), high1[:, :width], MAX)
             nc.vector.tensor_tensor(low2[:, :width], windows[k][:].indirect(second), low1[:, :width], MIN)
-            nc.vector.tensor_tensor(spans[k][:, nodes], high2[:, :width], low2[:, :width], SUBTRACT)
+            if start + width == V and k == BLOCKS - 1:
+                nc.vector.tensor_tensor(spans[k][:, nodes], high2[:, :width], low2[:, :width], SUBTRACT)
+                return
+            for left in range(0, width, BANK):
+                part = min(BANK, width - left)
+                difference = differences.tile([P, BANK], F32, name="difference")
+                nc.tensor.matmul(difference[:, :part], plus[:], high2[:, left : left + part], start=True, stop=False)
+                nc.tensor.matmul(difference[:, :part], minus[:], low2[:, left : left + part], start=False, stop=True)
+                nc.scalar.activation(spans[k][:, start + left : start + left + part], difference[:, :part], COPY)
 
         for k in range(BLOCKS - 1):
             look_up(k, 0, V)

@@ -15,7 +15,7 @@ GROUPS = M // P
 PER_COLUMN = 16
 BANK = 512
 
-PIECES = ((0, BANK), (BANK, BANK // 2), (BANK + BANK // 2, BANK // 2))
+PIECES = ((0, BANK), (BANK, 3 * BANK // 4), (BANK + 3 * BANK // 4, BANK // 4))
 
 FLOPS = 2 * ROWS * M * V
 
@@ -27,8 +27,7 @@ def tile_lookup_span_relu_kernel(tc, tab, x0, w, b, offs, out):
         tc.tile_pool(name="blocks", bufs=BLOCKS) as blocks,
         tc.tile_pool(name="work", bufs=2) as work,
         tc.tile_pool(name="results", bufs=2 * GROUPS) as results,
-        tc.psum_pool(name="differences", bufs=2) as differences,
-        tc.psum_pool(name="psum", bufs=6) as psum,
+        tc.psum_pool(name="psum", bufs=1) as psum,
     ):
         offsets = held.tile([P, 2 * V // PER_COLUMN], U16, name="offsets")
         nc.sync.dma_start(offsets[:], offs)
@@ -38,12 +37,10 @@ def tile_lookup_span_relu_kernel(tc, tab, x0, w, b, offs, out):
             rows = slice(k * P, (k + 1) * P)
             window = blocks.tile([P, COLS], F32, name="window")
             own = blocks.tile([P, V], F32, name="own")
-            if k == 0:
-                nc.scalar.dma_start(window[:, : COLS // 2], tab[rows, : COLS // 2])
-                nc.sync.dma_start(window[:, COLS // 2 :], tab[rows, COLS // 2 :])
-            else:
-                nc.sync.dma_start(window[:], tab[rows, :])
-            nc.scalar.dma_start(own[:], x0[rows, :])
+            nc.scalar.dma_start(window[:, : COLS // 2], tab[rows, : COLS // 2])
+            nc.sync.dma_start(window[:, COLS // 2 :], tab[rows, COLS // 2 :])
+            nc.scalar.dma_start(own[:, : V // 2], x0[rows, : V // 2])
+            nc.sync.dma_start(own[:, V // 2 :], x0[rows, V // 2 :])
             windows.append(window)
             owns.append(own)
 
@@ -57,6 +54,8 @@ def tile_lookup_span_relu_kernel(tc, tab, x0, w, b, offs, out):
         minus = held.tile([P, P], F32, name="minus")
         make_identity(nc, plus[:])
         nc.gpsimd.tensor_scalar_mul(minus[:], plus[:], -1.0)
+
+        banks = [psum.tile([P, BANK], F32, name=f"bank_{i}") for i in range(2 * GROUPS)]
 
         spans = [blocks.tile([P, V], BF16, name="span") for k in range(BLOCKS)]
 
@@ -72,36 +71,47 @@ def tile_lookup_span_relu_kernel(tc, tab, x0, w, b, offs, out):
             nc.vector.tensor_tensor(low1[:, :width], windows[k][:].indirect(first), owns[k][:, nodes], MIN)
             nc.vector.tensor_tensor(high2[:, :width], windows[k][:].indirect(second), high1[:, :width], MAX)
             nc.vector.tensor_tensor(low2[:, :width], windows[k][:].indirect(second), low1[:, :width], MIN)
-            if start + width == V and k == BLOCKS - 1:
+            if k == BLOCKS - 1:
                 nc.vector.tensor_tensor(spans[k][:, nodes], high2[:, :width], low2[:, :width], SUBTRACT)
                 return
-            for left in range(0, width, BANK):
-                part = min(BANK, width - left)
-                difference = differences.tile([P, BANK], F32, name="difference")
-                nc.tensor.matmul(difference[:, :part], plus[:], high2[:, left : left + part], start=True, stop=False)
-                nc.tensor.matmul(difference[:, :part], minus[:], low2[:, left : left + part], start=False, stop=True)
-                nc.scalar.activation(spans[k][:, start + left : start + left + part], difference[:, :part], COPY)
+            for h in range(V // BANK):
+                half = slice(h * BANK, (h + 1) * BANK)
+                difference = banks[h - V // BANK]
+                nc.tensor.matmul(difference[:], plus[:], high2[:, half], start=True, stop=False)
+                nc.tensor.matmul(difference[:], minus[:], low2[:, half], start=False, stop=True)
+                nc.scalar.activation(spans[k][:, half], difference[:], COPY)
+
+        def add_products(i, k):
+            start, width = PIECES[i]
+            for g in range(GROUPS):
+                nc.tensor.matmul(
+                    banks[i % 2 * GROUPS + g][:, :width],
+                    weights[:, k, g * P : (g + 1) * P],
+                    spans[k][:, start : start + width],
+                    start=(k == 0),
+                    stop=(k == BLOCKS - 1),
+                )
+
+        def finish(i):
+            start, width = PIECES[i]
+            look_up(BLOCKS - 1, start, width)
+            add_products(i, BLOCKS - 1)
+            for g in range(GROUPS):
+                total = banks[i % 2 * GROUPS + g][:, :width]
+                result = results.tile([P, BANK], F32, name="result")
+                if i == len(PIECES) - 1 and g % 2 == 1:
+                    nc.vector.tensor_scalar(result[:, :width], total, bias[:, g : g + 1], 0.0, ADD, MAX)
+                else:
+                    nc.scalar.activation(result[:, :width], total, RELU, bias=bias[:, g : g + 1])
+                nc.sync.dma_start(out[g * P : (g + 1) * P, start : start + width], result[:, :width])
 
         for k in range(BLOCKS - 1):
             look_up(k, 0, V)
-
-        for start, width in PIECES:
-            look_up(BLOCKS - 1, start, width)
-            nodes = slice(start, start + width)
-            sums = [psum.tile([P, BANK], F32, name="sum") for g in range(GROUPS)]
-            for k in range(BLOCKS):
-                for g in range(GROUPS):
-                    nc.tensor.matmul(
-                        sums[g][:, :width],
-                        weights[:, k, g * P : (g + 1) * P],
-                        spans[k][:, nodes],
-                        start=(k == 0),
-                        stop=(k == BLOCKS - 1),
-                    )
-            for g in range(GROUPS):
-                result = results.tile([P, BANK], F32, name="result")
-                if start + width == V and g % 2 == 1:
-                    nc.vector.tensor_scalar(result[:, :width], sums[g][:, :width], bias[:, g : g + 1], 0.0, ADD, MAX)
-                else:
-                    nc.scalar.activation(result[:, :width], sums[g][:, :width], RELU, bias=bias[:, g : g + 1])
-                nc.sync.dma_start(out[g * P : (g + 1) * P, nodes], result[:, :width])
+            add_products(0, k)
+        for k in range(BLOCKS - 1):
+            add_products(1, k)
+        finish(0)
+        for k in range(BLOCKS - 1):
+            add_products(2, k)
+        finish(1)
+        finish(2)

import concourse.mybir as mybir
from concourse.masks import make_identity

F32, BF16, U16 = mybir.dt.float32, mybir.dt.bfloat16, mybir.dt.uint16
MAX, MIN, SUBTRACT = mybir.AluOpType.max, mybir.AluOpType.min, mybir.AluOpType.subtract
ADD = mybir.AluOpType.add
COPY, RELU = mybir.ActivationFunctionType.Copy, mybir.ActivationFunctionType.Relu

P = 128
ROWS, COLS = 512, 2048
V = 1024
M = 512
BLOCKS = ROWS // P
GROUPS = M // P
PER_COLUMN = 16
BANK = 512

PIECES = ((0, BANK), (BANK, 3 * BANK // 4), (BANK + 3 * BANK // 4, BANK // 4))

FLOPS = 2 * ROWS * M * V


def tile_lookup_span_relu_kernel(tc, tab, x0, w, b, offs, out):
    nc = tc.nc
    with (
        tc.tile_pool(name="held", bufs=1) as held,
        tc.tile_pool(name="blocks", bufs=BLOCKS) as blocks,
        tc.tile_pool(name="work", bufs=2) as work,
        tc.tile_pool(name="results", bufs=2 * GROUPS) as results,
        tc.psum_pool(name="psum", bufs=1) as psum,
    ):
        offsets = held.tile([P, 2 * V // PER_COLUMN], U16, name="offsets")
        nc.sync.dma_start(offsets[:], offs)

        windows, owns = [], []
        for k in range(BLOCKS):
            rows = slice(k * P, (k + 1) * P)
            window = blocks.tile([P, COLS], F32, name="window")
            own = blocks.tile([P, V], F32, name="own")
            nc.scalar.dma_start(window[:, : COLS // 2], tab[rows, : COLS // 2])
            nc.sync.dma_start(window[:, COLS // 2 :], tab[rows, COLS // 2 :])
            nc.scalar.dma_start(own[:, : V // 2], x0[rows, : V // 2])
            nc.sync.dma_start(own[:, V // 2 :], x0[rows, V // 2 :])
            windows.append(window)
            owns.append(own)

        weights = held.tile([P, BLOCKS, M], BF16, name="weights")
        nc.scalar.dma_start(weights[:], w.rearrange("(k p) m -> p k m", p=P))
        bias = held.tile([P, GROUPS], F32, name="bias")
        with nc.allow_non_contiguous_dma(reason="512 single values, once"):
            nc.scalar.dma_start(bias[:], b.rearrange("(g p) one -> p (g one)", p=P))

        plus = held.tile([P, P], F32, name="plus")
        minus = held.tile([P, P], F32, name="minus")
        make_identity(nc, plus[:])
        nc.gpsimd.tensor_scalar_mul(minus[:], plus[:], -1.0)

        banks = [psum.tile([P, BANK], F32, name=f"bank_{i}") for i in range(2 * GROUPS)]

        spans = [blocks.tile([P, V], BF16, name="span") for k in range(BLOCKS)]

        def look_up(k, start, width):
            nodes = slice(start, start + width)
            first = offsets[:, start // PER_COLUMN : (start + width) // PER_COLUMN]
            second = offsets[:, (V + start) // PER_COLUMN : (V + start + width) // PER_COLUMN]
            high1 = work.tile([P, V], F32, name="high1")
            low1 = work.tile([P, V], F32, name="low1")
            high2 = work.tile([P, V], F32, name="high2")
            low2 = work.tile([P, V], F32, name="low2")
            nc.vector.tensor_tensor(high1[:, :width], windows[k][:].indirect(first), owns[k][:, nodes], MAX)
            nc.vector.tensor_tensor(low1[:, :width], windows[k][:].indirect(first), owns[k][:, nodes], MIN)
            nc.vector.tensor_tensor(high2[:, :width], windows[k][:].indirect(second), high1[:, :width], MAX)
            nc.vector.tensor_tensor(low2[:, :width], windows[k][:].indirect(second), low1[:, :width], MIN)
            if k == BLOCKS - 1:
                nc.vector.tensor_tensor(spans[k][:, nodes], high2[:, :width], low2[:, :width], SUBTRACT)
                return
            for h in range(V // BANK):
                half = slice(h * BANK, (h + 1) * BANK)
                difference = banks[h - V // BANK]
                nc.tensor.matmul(difference[:], plus[:], high2[:, half], start=True, stop=False)
                nc.tensor.matmul(difference[:], minus[:], low2[:, half], start=False, stop=True)
                nc.scalar.activation(spans[k][:, half], difference[:], COPY)

        def add_products(i, k):
            start, width = PIECES[i]
            for g in range(GROUPS):
                nc.tensor.matmul(
                    banks[i % 2 * GROUPS + g][:, :width],
                    weights[:, k, g * P : (g + 1) * P],
                    spans[k][:, start : start + width],
                    start=(k == 0),
                    stop=(k == BLOCKS - 1),
                )

        def finish(i):
            start, width = PIECES[i]
            look_up(BLOCKS - 1, start, width)
            add_products(i, BLOCKS - 1)
            for g in range(GROUPS):
                total = banks[i % 2 * GROUPS + g][:, :width]
                result = results.tile([P, BANK], F32, name="result")
                if i == len(PIECES) - 1 and g % 2 == 1:
                    nc.vector.tensor_scalar(result[:, :width], total, bias[:, g : g + 1], 0.0, ADD, MAX)
                else:
                    nc.scalar.activation(result[:, :width], total, RELU, bias=bias[:, g : g + 1])
                nc.sync.dma_start(out[g * P : (g + 1) * P, start : start + width], result[:, :width])

        for k in range(BLOCKS - 1):
            look_up(k, 0, V)
            add_products(0, k)
        for k in range(BLOCKS - 1):
            add_products(1, k)
        finish(0)
        for k in range(BLOCKS - 1):
            add_products(2, k)
        finish(1)
        finish(2)
